import numpy as np
import ml_dtypes


def mxq(x, axis, fmt="e4m3"):
    dtype, down = {"e4m3": (ml_dtypes.float8_e4m3fn, 7), "e5m2": (ml_dtypes.float8_e5m2, 14)}[fmt]
    v = np.moveaxis(np.asarray(x, np.float32).astype(ml_dtypes.bfloat16).astype(np.float64), axis, -1)
    blocks = v.reshape(v.shape[:-1] + (-1, 32))
    amax = np.abs(blocks).max(-1, keepdims=True)
    byte = np.maximum(np.where(amax > 0, np.frexp(amax)[1] - 1 + 127, 0) - down, 1)
    scale = np.exp2(byte - 127.0)
    codes = (blocks / scale).astype(np.float32).astype(dtype).astype(np.float64)
    return np.moveaxis((codes * scale).reshape(v.shape), -1, axis)


WIDE = False


def mx_kscale(k):
    if not WIDE:
        return np.ones(k)
    levels = np.array([10, -10, 5, -5, 0])
    if k % 512:
        return np.exp2(np.random.permutation(np.resize(levels, k // 32))).repeat(32)
    a = np.empty((k // 512, 16))
    for p in range(k // 512):
        a[p, :8] = np.random.permutation(np.resize(levels, 8))
        for g in range(8):
            far = levels[np.abs(levels - a[p, g]) >= 10]
            a[p, g + 8] = far[np.random.randint(len(far))]
    return np.exp2(a.ravel()).repeat(32)


BF16 = ml_dtypes.bfloat16


def bf(x):
    return np.asarray(x, np.float32).astype(BF16)


def f64(x):
    return np.asarray(x).astype(np.float64)


E2M1 = np.array([0.0, 0.5, 1.0, 1.5, 2.0, 3.0, 4.0, 6.0, -0.0, -0.5, -1.0, -1.5, -2.0, -3.0, -4.0, -6.0])


def pack_weight(w, fmt):
    k, n = w.shape
    w = f64(bf(w)).reshape(k // 32, 32, n)
    amax = np.abs(w).max(1)
    if fmt == "e4m3":
        byte = np.frexp(amax)[1] - 1 + 127 - 7
    else:
        mant, ex = np.frexp(amax / 6.0)
        byte = np.where(mant > 0.5, ex, ex - 1) + 127
    byte = np.clip(np.where(amax > 0, byte, 1), 1, 254)
    scaled = (w * np.exp2(127.0 - byte)[:, None, :]).reshape(k, n).astype(np.float32)
    by_word = np.ascontiguousarray(scaled.reshape(k // 512, 128, 4, n).transpose(0, 1, 3, 2))
    if fmt == "e4m3":
        words = by_word.astype(ml_dtypes.float8_e4m3fn).view(np.uint8)
    else:
        c = by_word.astype(ml_dtypes.float4_e2m1fn).view(np.uint8) & 0xF
        words = c[..., 0::2] | (c[..., 1::2] << 4)
    return np.ascontiguousarray(words), np.ascontiguousarray(byte.astype(np.uint8).reshape(k // 512, 16, n))


def unpack_weight(words, scales, fmt):
    g, p, n, _ = words.shape
    if fmt == "e4m3":
        vals = np.ascontiguousarray(words).view(ml_dtypes.float8_e4m3fn).astype(np.float64)
    else:
        nib = np.empty((g, p, n, 4), np.uint8)
        nib[..., 0::2] = words & 0xF
        nib[..., 1::2] = words >> 4
        vals = E2M1[nib]
    vals = vals * np.repeat(np.exp2(scales.astype(np.float64) - 127.0), 8, axis=1)[..., None]
    return vals.transpose(0, 1, 3, 2).reshape(g * 512, n)
def pack4(w):
    words, scales = pack_weight(w, "e2m1")
    return words.reshape(words.shape[0], 128, -1), scales


def unpack4(words, scales):
    return unpack_weight(words.reshape(words.shape[0], 128, -1, 2), scales, "e2m1")


M, K, R = 2048, 512, 512


def draw0():
    s = mx_kscale(K)
    u = mx_kscale(M)
    loads = np.random.standard_normal((M, K)) * s * u[:, None]
    lag_loads = 0.25 * np.random.standard_normal((K, M)) / np.sqrt(K) / s[:, None]
    gain = 1 + 0.1 * np.random.standard_normal(M)
    private = (4 + 0.5 * np.random.standard_normal(M)) * u
    readout = 2 * np.random.standard_normal((M, R)) / np.sqrt(M) / u[:, None]
    words, scales = pack4(readout)
    return {"loads": bf(loads),
            "lag_loads": bf(lag_loads),
            "gain": bf(gain),
            "private": bf(private),
            "readout_words": words,
            "readout_scales": scales}


def core(loads, lag_loads, gain, private, readout_words, readout_scales):
    a = mxq(f64(loads), 1, "e4m3")
    b = mxq(f64(lag_loads), 0, "e4m3")
    shared = a @ b
    cov = shared * f64(gain)[:, None] + f64(private)[:, None] * np.eye(M)
    w = unpack4(readout_words, readout_scales)
    return w.T @ mxq(cov, 0, "e4m3")


def e4m3fn_bytes(y):
    return np.clip(np.asarray(y, np.float64), -448.0, 448.0).astype(np.float32).astype(ml_dtypes.float8_e4m3fn).view(np.uint8)


def e4m3fn_values(b):
    return np.asarray(b, np.uint8).view(ml_dtypes.float8_e4m3fn).astype(np.float64)


def setup_inputs():
    d = draw0()
    x0 = np.asarray(d['lag_loads']).astype(np.float64)
    s = (np.max(np.abs(x0), axis=(1,), keepdims=True) / 448.0).astype(np.float32)
    out = {}
    for k, v in d.items():
        if k == 'lag_loads':
            out['lag_loads_bytes'] = e4m3fn_bytes(x0 / s.astype(np.float64))
            out['lag_loads_scale'] = s
        else:
            out[k] = v
    return out


def reference(loads, lag_loads_bytes, lag_loads_scale, gain, private, readout_words, readout_scales):
    return core(loads, e4m3fn_values(lag_loads_bytes) * lag_loads_scale.astype(np.float64), gain, private, readout_words, readout_scales)

@@ -1,0 +1,414 @@
+from contextlib import ExitStack
+
+import concourse.mybir as mybir
+from concourse.masks import make_identity
+
+F32 = mybir.dt.float32
+BF16 = mybir.dt.bfloat16
+U32 = mybir.dt.uint32
+I32 = mybir.dt.int32
+U8 = mybir.dt.uint8
+FP8 = mybir.dt.float8_e4m3fn
+FP8X4 = mybir.dt.float8_e4m3fn_x4
+FP4X4 = mybir.dt.float4_e2m1fn_x4
+ALU = mybir.AluOpType
+ACT = mybir.ActivationFunctionType
+
+M, K, R = 2048, 512, 512
+FLOPS = 2 * M * K * M + 2 * R * M * M
+
+P = 128
+BLOCK_ORDER = (3, 0, 1, 2)
+
+
+def tile_spike_covariance_readout_s13_kernel(
+    tc, loads, lag_bytes, lag_scale, gain, private, w_words, w_scales, out
+):
+    nc = tc.nc
+    with ExitStack() as ctx:
+        keep = ctx.enter_context(tc.tile_pool(name="keep", bufs=1))
+        work = ctx.enter_context(tc.tile_pool(name="work", bufs=3))
+        psum = ctx.enter_context(tc.psum_pool(name="psum", bufs=4))
+        ctx.enter_context(tc.manual_schedule())
+
+        lagsc = keep.tile([P, 4], F32, name="lagsc")
+        nc.scalar.dma_start(out=lagsc[:], in_=lag_scale.rearrange("(p t) o -> p (t o)", t=4))
+        gain_b = keep.tile([P, 4, 4], BF16, name="gain_b")
+        nc.scalar.dma_start(out=gain_b[:], in_=gain.rearrange("(g p t) -> p g t", p=P, t=4))
+        priv_b = keep.tile([P, 4, 4], BF16, name="priv_b")
+        nc.scalar.dma_start(out=priv_b[:], in_=private.rearrange("(g p t) -> p g t", p=P, t=4))
+
+        lag_view = lag_bytes.rearrange("(p t) j -> p t j", t=4)
+        lag_raw = {}
+        raw = {}
+
+        def load_lag(jb):
+            lraw = work.tile([P, 4, 512], U8, name="lraw", bufs=4, align_bytes=64)
+            nc.sync.dma_start(out=lraw[:], in_=lag_view[:, :, 512 * jb : 512 * jb + 512])
+            lag_raw[jb] = lraw
+
+        def load_loads(g):
+            rows = work.tile([P, 4, 512], BF16, name="rows", bufs=4, align_bytes=64)
+            nc.sync.dma_start(out=rows[:], in_=loads[512 * g : 512 * g + 512, :].rearrange("(m t) k -> m t k", t=4))
+            raw[g] = rows
+
+        load_lag(BLOCK_ORDER[0])
+        load_loads(0)
+        load_loads(1)
+        load_lag(BLOCK_ORDER[1])
+        load_loads(2)
+        load_loads(3)
+        w_sb = keep.tile([P, 4, 1024], U8, name="w_sb", align_bytes=64)
+        nc.sync.dma_start(out=w_sb[:], in_=w_words.rearrange("g p n -> p g n"))
+        ws_sb = keep.tile([P, 4, 512], U8, name="ws_sb", align_bytes=64)
+        nc.vector.memset(ws_sb[:].rearrange("p g n -> p (g n)").bitcast(I32), 0)
+        ws_view = w_scales.bitcast(I32).rearrange("g q n -> q g n")
+        for quad in range(4):
+            nc.sync.dma_start(
+                out=ws_sb[32 * quad : 32 * quad + 4, :, :].bitcast(I32),
+                in_=ws_view[4 * quad : 4 * quad + 4, :, :],
+            )
+        load_lag(BLOCK_ORDER[2])
+        load_lag(BLOCK_ORDER[3])
+
+        warm = keep.tile([P, 1], F32, name="warm")
+        nc.gpsimd.memset(warm[:], 0.0)
+        warm2 = keep.tile([P, 1], F32, name="warm2")
+        nc.scalar.activation(out=warm2[:], in_=warm[:], func=ACT.Copy, scale=1.0)
+        ident = keep.tile([P, P], F32, name="ident")
+        make_identity(nc, ident[:])
+        gain_f = keep.tile([P, 16], F32, name="gain_f")
+        nc.gpsimd.tensor_copy(out=gain_f[:], in_=gain_b[:].rearrange("p g t -> p (g t)"))
+        priv_f = keep.tile([P, 16], F32, name="priv_f")
+        nc.gpsimd.tensor_copy(out=priv_f[:], in_=priv_b[:].rearrange("p g t -> p (g t)"))
+        diag = keep.tile([P, 16, P], BF16, name="diag")
+        for jb in BLOCK_ORDER:
+            for t in range(4):
+                i = 4 * jb + t
+                nc.gpsimd.tensor_scalar(
+                    out=diag[:, i, :], in0=ident[:], scalar1=priv_f[:, i : i + 1], scalar2=0.0, op0=ALU.mult, op1=ALU.add
+                )
+
+        lag_planes, lag_grp, lag_codes, lag_sc = {}, {}, {}, {}
+        ld_grp, ld_codes, ld_sc = {}, {}, {}
+
+        def lag_alloc(jb):
+            lpl = work.tile([P, 4, 512], BF16, name="lpl", bufs=2, align_bytes=64)
+            lgr = work.tile([P, 512, 4], BF16, name="lgr", bufs=2, align_bytes=64)
+            lco = work.tile([P, 512], U32, name="lco", bufs=2, align_bytes=64)
+            lsc = work.tile([P, 512], U8, name="lsc", bufs=2, align_bytes=64)
+            lag_planes[jb], lag_grp[jb], lag_codes[jb], lag_sc[jb] = lpl, lgr, lco, lsc
+
+        def lag_widen(jb, t, on_scalar):
+            src = lag_raw[jb][:, t, :].bitcast(FP8)
+            dst = lag_planes[jb][:, t, :]
+            if on_scalar:
+                nc.scalar.activation(out=dst, in_=src, func=ACT.Copy, scale=lagsc[:, t : t + 1])
+            else:
+                nc.vector.tensor_scalar(out=dst, in0=src, scalar1=lagsc[:, t : t + 1], scalar2=None, op0=ALU.mult)
+
+        def lag_interleave(jb, h):
+            src = lag_planes[jb][:, :, 256 * h : 256 * h + 256].rearrange("p t (q m s) -> p q m t s", q=2, s=4)
+            dst = lag_grp[jb][:, 256 * h : 256 * h + 256, :].rearrange("p (q s m) t -> p q m t s", q=2, s=4)
+            nc.vector.tensor_copy(out=dst, in_=src)
+
+        def lag_quant(jb, h):
+            c = slice(256 * h, 256 * h + 256)
+            nc.vector.quantize_mx(
+                out=lag_codes[jb][:, c].bitcast(FP8X4),
+                scales=lag_sc[jb][:, c],
+                in_=lag_grp[jb][:, c, :].rearrange("p c t -> p (c t)"),
+            )
+
+        turned = {}
+
+        def loads_turn(g):
+            lg = work.tile([P, 512, 4], BF16, name="lg", bufs=2, align_bytes=64)
+            ld_grp[g] = lg
+            turned[g] = []
+            for h in range(2):
+                o_bank = psum.tile([P, 512], F32, name="o_bank")
+                view = o_bank[:].rearrange("p (t u m) -> p t u m", t=2, u=2)
+                for tt in range(2):
+                    words = raw[g][:, 2 * h + tt, :].bitcast(F32)
+                    for u in range(2):
+                        nc.tensor.transpose(view[:, tt, u, :], words[:, u:256:2], ident[:])
+                turned[g].append(o_bank)
+
+        def loads_exit(g, h, on_scalar):
+            src = turned[g][h][:].rearrange("p (t u m) -> p t m u", t=2, u=2)
+            dst = (
+                ld_grp[g][:, 256 * h : 256 * h + 256, :]
+                .rearrange("p c t -> p (c t)")
+                .bitcast(F32)
+                .rearrange("p (t m u) -> p t m u", t=2, u=2)
+            )
+            if on_scalar:
+                nc.scalar.copy(out=dst, in_=src)
+            else:
+                nc.vector.tensor_copy(out=dst, in_=src)
+
+        def loads_quant(g):
+            lc = work.tile([P, 512], U32, name="lc", bufs=4, align_bytes=64)
+            ls = work.tile([P, 512], U8, name="ls", bufs=4, align_bytes=64)
+            ld_codes[g], ld_sc[g] = lc, ls
+            nc.vector.quantize_mx(
+                out=lc[:].bitcast(FP8X4), scales=ls[:], in_=ld_grp[g][:].rearrange("p c t -> p (c t)")
+            )
+
+        units = [(jb, g) for jb in BLOCK_ORDER[:3] for g in range(4)] + [(BLOCK_ORDER[3], q) for q in range(4)]
+        NU = len(units)
+        WIDE = 12
+        banks, planes, grouped, codes, scales = {}, {}, {}, {}, {}
+        o_banks = {}
+
+        def on_vector(n, g):
+            return g == 1 or (n == NU - 1 and g == 3)
+
+        def s_pass(n, x):
+            jb, y = units[n]
+            s_bank = psum.tile([P, 512], F32, name="s_bank")
+            banks[n, x] = s_bank
+            if n < WIDE:
+                nc.tensor.matmul_mx(
+                    out=s_bank[:],
+                    lhsT=ld_codes[y][:, 128 * x : 128 * x + 128].bitcast(FP8X4),
+                    lhsT_scale=ld_sc[y][:, 128 * x : 128 * x + 128],
+                    rhs=lag_codes[jb][:].bitcast(FP8X4),
+                    rhs_scale=lag_sc[jb][:],
+                    start=True,
+                    stop=True,
+                )
+            else:
+                for t in range(4):
+                    nc.tensor.matmul_mx(
+                        out=s_bank[:, 128 * t : 128 * t + 128],
+                        lhsT=ld_codes[x][:, 128 * t : 128 * t + 128].bitcast(FP8X4),
+                        lhsT_scale=ld_sc[x][:, 128 * t : 128 * t + 128],
+                        rhs=lag_codes[jb][:, 128 * y : 128 * y + 128].bitcast(FP8X4),
+                        rhs_scale=lag_sc[jb][:, 128 * y : 128 * y + 128],
+                        start=True,
+                        stop=True,
+                    )
+
+        def x_alloc(n):
+            pl = work.tile([P, 2048], BF16, name="pl", bufs=3, align_bytes=64)
+            gr = work.tile([P, 2048], BF16, name="gr", bufs=3, align_bytes=64)
+            co = work.tile([P, 512], U32, name="co", bufs=3, align_bytes=64)
+            sc = work.tile([P, 512], U8, name="sc", bufs=3, align_bytes=64)
+            planes[n], grouped[n], codes[n], scales[n] = pl, gr, co, sc
+
+        def pieces(t):
+            return [(a, b) for a, b in ((0, 32 * t), (32 * t + 32, 128)) if b > a]
+
+        def x_scalar(n, x):
+            jb, y = units[n]
+            bank = banks[n, x]
+            if n < WIDE:
+                g, t = y, x
+                col = gain_f[:, 4 * g + t : 4 * g + t + 1]
+                dst = planes[n][:, 512 * t : 512 * t + 512]
+                if g != jb:
+                    nc.scalar.activation(out=dst, in_=bank[:], func=ACT.Copy, scale=col)
+                else:
+                    b4 = bank[:].rearrange("p (q c) -> p q c", q=4)
+                    d4 = dst.rearrange("p (q c) -> p q c", q=4)
+                    for a, b in pieces(t):
+                        nc.scalar.activation(out=d4[:, :, a:b], in_=b4[:, :, a:b], func=ACT.Copy, scale=col)
+            else:
+                g = x
+                if on_vector(n, g):
+                    return
+                for t in range(4):
+                    col = gain_f[:, 4 * g + t : 4 * g + t + 1]
+                    for a, b in pieces(t) if g == jb else [(0, 128)]:
+                        nc.scalar.activation(
+                            out=planes[n][:, 512 * g + 128 * t + a : 512 * g + 128 * t + b],
+                            in_=bank[:, 128 * t + a : 128 * t + b],
+                            func=ACT.Copy,
+                            scale=col,
+                        )
+
+        def x_vector(n, x):
+            jb, y = units[n]
+            bank = banks[n, x]
+            if n < WIDE:
+                g, t = y, x
+                if g != jb:
+                    return
+                i = 4 * g + t
+                w = slice(32 * t, 32 * t + 32)
+                nc.vector.scalar_tensor_tensor(
+                    out=planes[n][:, 512 * t : 512 * t + 512].rearrange("p (q c) -> p q c", q=4)[:, :, w],
+                    in0=bank[:].rearrange("p (q c) -> p q c", q=4)[:, :, w],
+                    scalar=gain_f[:, i : i + 1],
+                    in1=diag[:, i, :].rearrange("p (q c) -> p q c", q=4),
+                    op0=ALU.mult,
+                    op1=ALU.add,
+                )
+            else:
+                g = x
+                if on_vector(n, g):
+                    nc.vector.tensor_tensor(
+                        out=grouped[n][:, 512 * g : 512 * g + 512].rearrange("p (c t) -> p c t", t=4),
+                        in0=bank[:].rearrange("p (t c) -> p c t", t=4),
+                        in1=gain_f[:, 4 * g : 4 * g + 4].unsqueeze(1).to_broadcast([P, 128, 4]),
+                        op=ALU.mult,
+                    )
+                elif g == jb:
+                    for t in range(4):
+                        i = 4 * g + t
+                        lo = 128 * t + 32 * t
+                        nc.vector.scalar_tensor_tensor(
+                            out=planes[n][:, 512 * g + lo : 512 * g + lo + 32],
+                            in0=bank[:, lo : lo + 32],
+                            scalar=gain_f[:, i : i + 1],
+                            in1=diag[:, i, 32 * y : 32 * y + 32],
+                            op0=ALU.mult,
+                            op1=ALU.add,
+                        )
+
+        def interleave(n, h):
+            if n < WIDE:
+                src = planes[n][:].rearrange("p (t c) -> p t c", t=4)[:, :, 256 * h : 256 * h + 256]
+                dst = grouped[n][:, 1024 * h : 1024 * h + 1024]
+                nc.vector.tensor_copy(
+                    out=dst.rearrange("p (c i t) -> p c t i", i=4, t=4), in_=src.rearrange("p t (c i) -> p c t i", i=4)
+                )
+            else:
+                for g in (2 * h, 2 * h + 1):
+                    if not on_vector(n, g):
+                        nc.vector.tensor_copy(
+                            out=grouped[n][:, 512 * g : 512 * g + 512].rearrange("p (c i t) -> p c t i", i=4, t=4),
+                            in_=planes[n][:, 512 * g : 512 * g + 512].rearrange("p (t c i) -> p c t i", t=4, i=4),
+                        )
+
+        def quant(n, h):
+            c = slice(256 * h, 256 * h + 256)
+            nc.vector.quantize_mx(
+                out=codes[n][:, c].bitcast(FP8X4),
+                scales=scales[n][:, c],
+                in_=grouped[n][:, 1024 * h : 1024 * h + 1024],
+            )
+
+        def w_op(g, r):
+            return w_sb[:, g, 256 * r : 256 * r + 256].bitcast(FP4X4), ws_sb[:, g, 128 * r : 128 * r + 128]
+
+        def o_pass(n, r):
+            jb, y = units[n]
+            if n < WIDE:
+                if y == 0:
+                    o_bank = psum.tile([P, 512], F32, name="o_bank")
+                    o_banks[n // 4, r] = o_bank
+                wc, ws = w_op(y, r)
+                nc.tensor.matmul_mx(
+                    out=o_banks[n // 4, r][:],
+                    lhsT=wc,
+                    lhsT_scale=ws,
+                    rhs=codes[n][:].bitcast(FP8X4),
+                    rhs_scale=scales[n][:],
+                    start=(y == 0),
+                    stop=(y == 3),
+                )
+            else:
+                if r == 0:
+                    o_bank = psum.tile([P, 512], F32, name="o_bank")
+                    o_banks[n, 0] = o_bank
+                for g in range(4):
+                    wc, ws = w_op(g, r)
+                    nc.tensor.matmul_mx(
+                        out=o_banks[n, 0][:, 128 * r : 128 * r + 128],
+                        lhsT=wc,
+                        lhsT_scale=ws,
+                        rhs=codes[n][:, 128 * g : 128 * g + 128].bitcast(FP8X4),
+                        rhs_scale=scales[n][:, 128 * g : 128 * g + 128],
+                        start=(g == 0),
+                        stop=(g == 3),
+                    )
+
+        def o_exit(k, r):
+            jb = BLOCK_ORDER[k]
+            ot = work.tile([P, 512], F32, name="ot", bufs=4)
+            nc.scalar.copy(
+                out=ot[:].rearrange("p (q m s) -> p q m s", q=4, s=4),
+                in_=o_banks[k, r][:].rearrange("p (q s m) -> p q m s", q=4, s=4),
+            )
+            nc.sync.dma_start(out=out[128 * r : 128 * r + 128, 512 * jb : 512 * jb + 512], in_=ot[:])
+
+        def o_exit_narrow(n):
+            jb, q = units[n]
+            j0 = 512 * jb + 128 * q
+            ot = work.tile([P, 512], F32, name="ot", bufs=4)
+            dst = ot[:].rearrange("p (r m s) -> p r m s", r=4, s=4)
+            src = o_banks[n, 0][:].rearrange("p (r s m) -> p r m s", r=4, s=4)
+            hbm = out[:, j0 : j0 + 128].rearrange("(r p) j -> p r j", p=P)
+            o3 = ot[:].rearrange("p (r j) -> p r j", r=4)
+            if n < NU - 1:
+                nc.scalar.copy(out=dst, in_=src)
+                nc.sync.dma_start(out=hbm, in_=o3)
+            else:
+                nc.scalar.copy(out=dst[:, 0:2], in_=src[:, 0:2])
+                nc.sync.dma_start(out=hbm[:, 0:2], in_=o3[:, 0:2])
+                nc.vector.tensor_copy(out=dst[:, 2:4], in_=src[:, 2:4])
+                nc.sync.dma_start(out=hbm[:, 2:4], in_=o3[:, 2:4])
+
+        jb0 = BLOCK_ORDER[0]
+        lag_alloc(jb0)
+        for t in range(4):
+            lag_widen(jb0, t, on_scalar=(t >= 2))
+        loads_turn(0)
+        for h in range(2):
+            loads_exit(0, h, on_scalar=True)
+        lag_interleave(jb0, 0)
+        lag_interleave(jb0, 1)
+        loads_quant(0)
+        lag_quant(jb0, 0)
+        lag_quant(jb0, 1)
+        for x in range(4):
+            s_pass(0, x)
+        loads_turn(1)
+        for h in range(2):
+            loads_exit(1, h, on_scalar=True)
+        loads_quant(1)
+
+        for n in range(NU + 2):
+            k = n // 4
+            if n < NU:
+                x_alloc(n)
+            if n in (0, 1):
+                loads_turn(n + 2)
+            if 1 <= n <= NU:
+                interleave(n - 1, 0)
+            for x in range(4):
+                if n < NU:
+                    x_scalar(n, x)
+                    x_vector(n, x)
+                if n in (6, 10, 14):
+                    o_exit((n - 6) // 4, x)
+                if n in (0, 1) and x in (1, 2):
+                    loads_exit(n + 2, x - 1, on_scalar=True)
+                if n in (0, 1) and x == 2:
+                    loads_quant(n + 2)
+                if n + 1 < NU:
+                    s_pass(n + 1, x)
+                if 0 <= n - 2:
+                    o_pass(n - 2, x)
+                if x == 1 and 1 <= n <= NU:
+                    interleave(n - 1, 1)
+            if n < 12:
+                jb = BLOCK_ORDER[k + 1]
+                if n % 4 == 0:
+                    lag_alloc(jb)
+                    for t in range(4):
+                        lag_widen(jb, t, on_scalar=False)
+                elif n % 4 == 1:
+                    lag_interleave(jb, 0)
+                    lag_interleave(jb, 1)
+                elif n % 4 == 2:
+                    lag_quant(jb, 0)
+                    lag_quant(jb, 1)
+            if 1 <= n <= NU:
+                quant(n - 1, 0)
+                quant(n - 1, 1)
+            if n - 2 >= WIDE:
+                o_exit_narrow(n - 2)

@@ -19,6 +19,7 @@ FLOPS = 2 * M * K * M + 2 * R * M * M
 
 P = 128
 BLOCK_ORDER = (3, 0, 1, 2)
+PITCH = 544
 
 
 def tile_spike_covariance_readout_s13_kernel(
@@ -47,17 +48,20 @@ def tile_spike_covariance_readout_s13_kernel(
             nc.sync.dma_start(out=lraw[:], in_=lag_view[:, :, 512 * jb : 512 * jb + 512])
             lag_raw[jb] = lraw
 
-        def load_loads(g):
+        def load_loads(g, parts):
             rows = work.tile([P, 4, 512], BF16, name="rows", bufs=4, align_bytes=64)
-            nc.sync.dma_start(out=rows[:], in_=loads[512 * g : 512 * g + 512, :].rearrange("(m t) k -> m t k", t=4))
+            src = loads[512 * g : 512 * g + 512, :].rearrange("(m t) k -> m t k", t=4)
+            step = 4 // parts
+            for a in range(0, 4, step):
+                nc.sync.dma_start(out=rows[:, a : a + step, :], in_=src[:, a : a + step, :])
             raw[g] = rows
 
         load_lag(BLOCK_ORDER[0])
-        load_loads(0)
-        load_loads(1)
+        load_loads(0, 2)
+        load_loads(1, 1)
         load_lag(BLOCK_ORDER[1])
-        load_loads(2)
-        load_loads(3)
+        load_loads(2, 1)
+        load_loads(3, 1)
         w_sb = keep.tile([P, 4, 1024], U8, name="w_sb", align_bytes=64)
         nc.sync.dma_start(out=w_sb[:], in_=w_words.rearrange("g p n -> p g n"))
         ws_sb = keep.tile([P, 4, 512], U8, name="ws_sb", align_bytes=64)
@@ -75,6 +79,8 @@ def tile_spike_covariance_readout_s13_kernel(
         nc.gpsimd.memset(warm[:], 0.0)
         warm2 = keep.tile([P, 1], F32, name="warm2")
         nc.scalar.activation(out=warm2[:], in_=warm[:], func=ACT.Copy, scale=1.0)
+        dmini = keep.tile([P, 4, 128, 4], BF16, name="dmini")
+        nc.gpsimd.memset(dmini[:].rearrange("p q c t -> p (q c t)").bitcast(I32), 0)
         ident = keep.tile([P, P], F32, name="ident")
         make_identity(nc, ident[:])
         gain_f = keep.tile([P, 16], F32, name="gain_f")
@@ -82,12 +88,22 @@ def tile_spike_covariance_readout_s13_kernel(
         priv_f = keep.tile([P, 16], F32, name="priv_f")
         nc.gpsimd.tensor_copy(out=priv_f[:], in_=priv_b[:].rearrange("p g t -> p (g t)"))
         diag = keep.tile([P, 16, P], BF16, name="diag")
-        for jb in BLOCK_ORDER:
+        for jb in BLOCK_ORDER[:3]:
             for t in range(4):
                 i = 4 * jb + t
                 nc.gpsimd.tensor_scalar(
                     out=diag[:, i, :], in0=ident[:], scalar1=priv_f[:, i : i + 1], scalar2=0.0, op0=ALU.mult, op1=ALU.add
                 )
+        for t in range(4):
+            i = 4 * BLOCK_ORDER[3] + t
+            nc.gpsimd.tensor_scalar(
+                out=dmini[:, :, 32 * t : 32 * t + 32, t],
+                in0=ident[:].rearrange("p (q m) -> p q m", q=4),
+                scalar1=priv_f[:, i : i + 1],
+                scalar2=0.0,
+                op0=ALU.mult,
+                op1=ALU.add,
+            )
 
         lag_planes, lag_grp, lag_codes, lag_sc = {}, {}, {}, {}
         ld_grp, ld_codes, ld_sc = {}, {}, {}
@@ -112,31 +128,31 @@ def tile_spike_covariance_readout_s13_kernel(
             dst = lag_grp[jb][:, 256 * h : 256 * h + 256, :].rearrange("p (q s m) t -> p q m t s", q=2, s=4)
             nc.vector.tensor_copy(out=dst, in_=src)
 
-        def lag_quant(jb, h):
-            c = slice(256 * h, 256 * h + 256)
+        def lag_quant(jb):
             nc.vector.quantize_mx(
-                out=lag_codes[jb][:, c].bitcast(FP8X4),
-                scales=lag_sc[jb][:, c],
-                in_=lag_grp[jb][:, c, :].rearrange("p c t -> p (c t)"),
+                out=lag_codes[jb][:].bitcast(FP8X4),
+                scales=lag_sc[jb][:],
+                in_=lag_grp[jb][:].rearrange("p c t -> p (c t)"),
             )
 
         turned = {}
 
-        def loads_turn(g):
-            lg = work.tile([P, 512, 4], BF16, name="lg", bufs=2, align_bytes=64)
-            ld_grp[g] = lg
-            turned[g] = []
-            for h in range(2):
-                o_bank = psum.tile([P, 512], F32, name="o_bank")
-                view = o_bank[:].rearrange("p (t u m) -> p t u m", t=2, u=2)
-                for tt in range(2):
-                    words = raw[g][:, 2 * h + tt, :].bitcast(F32)
-                    for u in range(2):
-                        nc.tensor.transpose(view[:, tt, u, :], words[:, u:256:2], ident[:])
-                turned[g].append(o_bank)
+        def loads_turn(g, h):
+            if h == 0:
+                lg = work.tile([P, 512, 4], BF16, name="lg", bufs=2, align_bytes=64)
+                lc = work.tile([P, 512], U32, name="lc", bufs=4, align_bytes=64)
+                ls = work.tile([P, 512], U8, name="ls", bufs=4, align_bytes=64)
+                ld_grp[g], ld_codes[g], ld_sc[g] = lg, lc, ls
+            o_bank = psum.tile([P, 512], F32, name="o_bank")
+            view = o_bank[:].rearrange("p (t u m) -> p t u m", t=2, u=2)
+            for tt in range(2):
+                words = raw[g][:, 2 * h + tt, :].bitcast(F32)
+                for u in range(2):
+                    nc.tensor.transpose(view[:, tt, u, :], words[:, u:256:2], ident[:])
+            turned[g, h] = o_bank
 
-        def loads_exit(g, h, on_scalar):
-            src = turned[g][h][:].rearrange("p (t u m) -> p t m u", t=2, u=2)
+        def loads_exit(g, h, on_scalar=True):
+            src = turned[g, h][:].rearrange("p (t u m) -> p t m u", t=2, u=2)
             dst = (
                 ld_grp[g][:, 256 * h : 256 * h + 256, :]
                 .rearrange("p c t -> p (c t)")
@@ -148,22 +164,24 @@ def tile_spike_covariance_readout_s13_kernel(
             else:
                 nc.vector.tensor_copy(out=dst, in_=src)
 
-        def loads_quant(g):
-            lc = work.tile([P, 512], U32, name="lc", bufs=4, align_bytes=64)
-            ls = work.tile([P, 512], U8, name="ls", bufs=4, align_bytes=64)
-            ld_codes[g], ld_sc[g] = lc, ls
+        def loads_quant(g, lo=0, hi=512):
             nc.vector.quantize_mx(
-                out=lc[:].bitcast(FP8X4), scales=ls[:], in_=ld_grp[g][:].rearrange("p c t -> p (c t)")
+                out=ld_codes[g][:, lo:hi].bitcast(FP8X4),
+                scales=ld_sc[g][:, lo:hi],
+                in_=ld_grp[g][:, lo:hi, :].rearrange("p c t -> p (c t)"),
             )
 
         units = [(jb, g) for jb in BLOCK_ORDER[:3] for g in range(4)] + [(BLOCK_ORDER[3], q) for q in range(4)]
         NU = len(units)
         WIDE = 12
-        banks, planes, grouped, codes, scales = {}, {}, {}, {}, {}
+        banks, planes, grouped, codes, scales, wins = {}, {}, {}, {}, {}, {}
         o_banks = {}
 
-        def on_vector(n, g):
-            return g == 1 or (n == NU - 1 and g == 3)
+        def direct(g):
+            return g == 1
+
+        def is_diag(n):
+            return n < WIDE and units[n][0] == units[n][1]
 
         def s_pass(n, x):
             jb, y = units[n]
@@ -192,103 +210,93 @@ def tile_spike_covariance_readout_s13_kernel(
                     )
 
         def x_alloc(n):
-            pl = work.tile([P, 2048], BF16, name="pl", bufs=3, align_bytes=64)
-            gr = work.tile([P, 2048], BF16, name="gr", bufs=3, align_bytes=64)
-            co = work.tile([P, 512], U32, name="co", bufs=3, align_bytes=64)
-            sc = work.tile([P, 512], U8, name="sc", bufs=3, align_bytes=64)
+            pl = work.tile([P, 4 * PITCH], BF16, name="pl", bufs=4, align_bytes=64)
+            gr = work.tile([P, 2048], BF16, name="gr", bufs=4, align_bytes=64)
+            co = work.tile([P, 512], U32, name="co", bufs=4, align_bytes=64)
+            sc = work.tile([P, 512], U8, name="sc", bufs=4, align_bytes=64)
             planes[n], grouped[n], codes[n], scales[n] = pl, gr, co, sc
+            if is_diag(n) or n >= WIDE:
+                win = work.tile([P, 4, 128], F32, name="win", bufs=2)
+                wins[n] = win
 
-        def pieces(t):
-            return [(a, b) for a, b in ((0, 32 * t), (32 * t + 32, 128)) if b > a]
+        def exit_scaled(dst, src, g, t):
+            nc.scalar.activation(out=dst, in_=src, func=ACT.Copy, scale=gain_f[:, 4 * g + t : 4 * g + t + 1])
 
         def x_scalar(n, x):
             jb, y = units[n]
             bank = banks[n, x]
             if n < WIDE:
                 g, t = y, x
-                col = gain_f[:, 4 * g + t : 4 * g + t + 1]
                 dst = planes[n][:, 512 * t : 512 * t + 512]
                 if g != jb:
-                    nc.scalar.activation(out=dst, in_=bank[:], func=ACT.Copy, scale=col)
+                    exit_scaled(dst, bank[:], g, t)
                 else:
                     b4 = bank[:].rearrange("p (q c) -> p q c", q=4)
                     d4 = dst.rearrange("p (q c) -> p q c", q=4)
-                    for a, b in pieces(t):
-                        nc.scalar.activation(out=d4[:, :, a:b], in_=b4[:, :, a:b], func=ACT.Copy, scale=col)
+                    lo, hi = 32 * t, 32 * t + 32
+                    exit_scaled(wins[n][:, t, :].rearrange("p (q c) -> p q c", q=4), b4[:, :, lo:hi], g, t)
+                    if t > 0:
+                        exit_scaled(d4[:, :, 0:lo], b4[:, :, 0:lo], g, t)
+                    if t < 3:
+                        exit_scaled(d4[:, :, hi:128], b4[:, :, hi:128], g, t)
             else:
                 g = x
-                if on_vector(n, g):
+                if direct(g):
                     return
                 for t in range(4):
-                    col = gain_f[:, 4 * g + t : 4 * g + t + 1]
-                    for a, b in pieces(t) if g == jb else [(0, 128)]:
-                        nc.scalar.activation(
-                            out=planes[n][:, 512 * g + 128 * t + a : 512 * g + 128 * t + b],
-                            in_=bank[:, 128 * t + a : 128 * t + b],
-                            func=ACT.Copy,
-                            scale=col,
-                        )
+                    c = slice(128 * t, 128 * t + 128)
+                    dst = wins[n][:, t, :] if g == jb else planes[n][:, 512 * g + 128 * t : 512 * g + 128 * t + 128]
+                    exit_scaled(dst, bank[:, c], g, t)
 
         def x_vector(n, x):
-            jb, y = units[n]
-            bank = banks[n, x]
-            if n < WIDE:
-                g, t = y, x
-                if g != jb:
-                    return
-                i = 4 * g + t
-                w = slice(32 * t, 32 * t + 32)
-                nc.vector.scalar_tensor_tensor(
-                    out=planes[n][:, 512 * t : 512 * t + 512].rearrange("p (q c) -> p q c", q=4)[:, :, w],
-                    in0=bank[:].rearrange("p (q c) -> p q c", q=4)[:, :, w],
-                    scalar=gain_f[:, i : i + 1],
-                    in1=diag[:, i, :].rearrange("p (q c) -> p q c", q=4),
-                    op0=ALU.mult,
-                    op1=ALU.add,
-                )
-            else:
-                g = x
-                if on_vector(n, g):
-                    nc.vector.tensor_tensor(
-                        out=grouped[n][:, 512 * g : 512 * g + 512].rearrange("p (c t) -> p c t", t=4),
-                        in0=bank[:].rearrange("p (t c) -> p c t", t=4),
-                        in1=gain_f[:, 4 * g : 4 * g + 4].unsqueeze(1).to_broadcast([P, 128, 4]),
-                        op=ALU.mult,
-                    )
-                elif g == jb:
-                    for t in range(4):
-                        i = 4 * g + t
-                        lo = 128 * t + 32 * t
-                        nc.vector.scalar_tensor_tensor(
-                            out=planes[n][:, 512 * g + lo : 512 * g + lo + 32],
-                            in0=bank[:, lo : lo + 32],
-                            scalar=gain_f[:, i : i + 1],
-                            in1=diag[:, i, 32 * y : 32 * y + 32],
-                            op0=ALU.mult,
-                            op1=ALU.add,
-                        )
+            if n < WIDE or not direct(x):
+                return
+            nc.vector.tensor_tensor(
+                out=grouped[n][:, 512 * x : 512 * x + 512].rearrange("p (c t) -> p c t", t=4),
+                in0=banks[n, x][:].rearrange("p (t c) -> p c t", t=4),
+                in1=gain_f[:, 4 * x : 4 * x + 4].unsqueeze(1).to_broadcast([P, 128, 4]),
+                op=ALU.mult,
+            )
 
-        def interleave(n, h):
+        def add_windows(n):
+            g = units[n][1]
+            nc.vector.tensor_tensor(
+                out=planes[n][:].rearrange("p (t c) -> p t c", t=4)[:, :, 0:512].rearrange("p t (q c) -> p t q c", q=4)[
+                    :, :, :, 0:32
+                ],
+                in0=wins[n][:].rearrange("p t (q c) -> p t q c", q=4),
+                in1=diag[:, 4 * g : 4 * g + 4, :].rearrange("p t (q c) -> p t q c", q=4),
+                op=ALU.add,
+            )
+
+        def interleave(n, gs=(0, 1, 2, 3)):
             if n < WIDE:
-                src = planes[n][:].rearrange("p (t c) -> p t c", t=4)[:, :, 256 * h : 256 * h + 256]
-                dst = grouped[n][:, 1024 * h : 1024 * h + 1024]
                 nc.vector.tensor_copy(
-                    out=dst.rearrange("p (c i t) -> p c t i", i=4, t=4), in_=src.rearrange("p t (c i) -> p c t i", i=4)
+                    out=grouped[n][:].rearrange("p (c i t) -> p c t i", i=4, t=4),
+                    in_=planes[n][:, 0:2048].rearrange("p (t c i) -> p c t i", t=4, i=4),
                 )
-            else:
-                for g in (2 * h, 2 * h + 1):
-                    if not on_vector(n, g):
-                        nc.vector.tensor_copy(
-                            out=grouped[n][:, 512 * g : 512 * g + 512].rearrange("p (c i t) -> p c t i", i=4, t=4),
-                            in_=planes[n][:, 512 * g : 512 * g + 512].rearrange("p (t c i) -> p c t i", t=4, i=4),
-                        )
+                return
+            jb, q = units[n]
+            for g in gs:
+                if direct(g):
+                    continue
+                dst = grouped[n][:, 512 * g : 512 * g + 512]
+                if g == jb:
+                    nc.vector.tensor_tensor(
+                        out=dst.rearrange("p (c t) -> p c t", t=4),
+                        in0=wins[n][:].rearrange("p t c -> p c t"),
+                        in1=dmini[:, q, :, :],
+                        op=ALU.add,
+                    )
+                else:
+                    nc.vector.tensor_copy(
+                        out=dst.rearrange("p (c i t) -> p c t i", i=4, t=4),
+                        in_=planes[n][:, 512 * g : 512 * g + 512].rearrange("p (t c i) -> p c t i", t=4, i=4),
+                    )
 
-        def quant(n, h):
-            c = slice(256 * h, 256 * h + 256)
+        def quant(n, lo=0, hi=512):
             nc.vector.quantize_mx(
-                out=codes[n][:, c].bitcast(FP8X4),
-                scales=scales[n][:, c],
-                in_=grouped[n][:, 1024 * h : 1024 * h + 1024],
+                out=codes[n][:, lo:hi].bitcast(FP8X4), scales=scales[n][:, lo:hi], in_=grouped[n][:, 4 * lo : 4 * hi]
             )
 
         def w_op(g, r):
@@ -328,7 +336,7 @@ def tile_spike_covariance_readout_s13_kernel(
 
         def o_exit(k, r):
             jb = BLOCK_ORDER[k]
-            ot = work.tile([P, 512], F32, name="ot", bufs=4)
+            ot = work.tile([P, 512], F32, name="ot", bufs=8)
             nc.scalar.copy(
                 out=ot[:].rearrange("p (q m s) -> p q m s", q=4, s=4),
                 in_=o_banks[k, r][:].rearrange("p (q s m) -> p q m s", q=4, s=4),
@@ -338,77 +346,127 @@ def tile_spike_covariance_readout_s13_kernel(
         def o_exit_narrow(n):
             jb, q = units[n]
             j0 = 512 * jb + 128 * q
-            ot = work.tile([P, 512], F32, name="ot", bufs=4)
+            ot = work.tile([P, 512], F32, name="ot", bufs=8)
             dst = ot[:].rearrange("p (r m s) -> p r m s", r=4, s=4)
             src = o_banks[n, 0][:].rearrange("p (r s m) -> p r m s", r=4, s=4)
             hbm = out[:, j0 : j0 + 128].rearrange("(r p) j -> p r j", p=P)
             o3 = ot[:].rearrange("p (r j) -> p r j", r=4)
-            if n < NU - 1:
-                nc.scalar.copy(out=dst, in_=src)
-                nc.sync.dma_start(out=hbm, in_=o3)
-            else:
-                nc.scalar.copy(out=dst[:, 0:2], in_=src[:, 0:2])
-                nc.sync.dma_start(out=hbm[:, 0:2], in_=o3[:, 0:2])
-                nc.vector.tensor_copy(out=dst[:, 2:4], in_=src[:, 2:4])
-                nc.sync.dma_start(out=hbm[:, 2:4], in_=o3[:, 2:4])
+            nc.scalar.copy(out=dst, in_=src)
+            nc.sync.dma_start(out=hbm, in_=o3)
+
+        def finish(n):
+            jb, q = units[n]
+            j0 = 512 * jb + 128 * q
+            accs = []
+            for r in range(4):
+                s_bank = psum.tile([P, 512], F32, name="s_bank")
+                accs.append(s_bank)
+            for g in range(4):
+                for r in range(4):
+                    wc, ws = w_op(g, r)
+                    nc.tensor.matmul_mx(
+                        out=accs[r][:, 0:128],
+                        lhsT=wc,
+                        lhsT_scale=ws,
+                        rhs=codes[n][:, 128 * g : 128 * g + 128].bitcast(FP8X4),
+                        rhs_scale=scales[n][:, 128 * g : 128 * g + 128],
+                        start=(g == 0),
+                        stop=(g == 3),
+                    )
+            ot = work.tile([P, 512], F32, name="ot", bufs=8)
+            o3 = ot[:].rearrange("p (r j) -> p r j", r=4)
+            hbm = out[:, j0 : j0 + 128].rearrange("(r p) j -> p r j", p=P)
+            for r in range(4):
+                dst = o3[:, r, :].rearrange("p (m s) -> p m s", s=4)
+                src = accs[r][:, 0:128].rearrange("p (s m) -> p m s", s=4)
+                if r % 2 == 0:
+                    nc.scalar.copy(out=dst, in_=src)
+                else:
+                    nc.vector.tensor_copy(out=dst, in_=src)
+                    nc.sync.dma_start(out=hbm[:, r - 1 : r + 1], in_=o3[:, r - 1 : r + 1])
 
         jb0 = BLOCK_ORDER[0]
         lag_alloc(jb0)
-        for t in range(4):
-            lag_widen(jb0, t, on_scalar=(t >= 2))
-        loads_turn(0)
-        for h in range(2):
-            loads_exit(0, h, on_scalar=True)
+        lag_widen(jb0, 3, True)
+        for t in range(3):
+            lag_widen(jb0, t, False)
+        loads_turn(0, 0)
+        loads_exit(0, 0)
+        loads_turn(0, 1)
+        loads_exit(0, 1)
         lag_interleave(jb0, 0)
         lag_interleave(jb0, 1)
-        loads_quant(0)
-        lag_quant(jb0, 0)
-        lag_quant(jb0, 1)
+        loads_quant(0, 0, 256)
+        lag_quant(jb0)
+        loads_quant(0, 256, 512)
+        for h in range(2):
+            loads_turn(1, h)
+            loads_exit(1, h)
+        lag_alloc(BLOCK_ORDER[1])
+        for t in range(4):
+            lag_widen(BLOCK_ORDER[1], t, False)
+        loads_quant(1)
         for x in range(4):
             s_pass(0, x)
-        loads_turn(1)
-        for h in range(2):
-            loads_exit(1, h, on_scalar=True)
-        loads_quant(1)
 
-        for n in range(NU + 2):
+        O_DELAY = 14
+        E_STEP = 16 + O_DELAY
+        for n in range(NU + 3):
             k = n // 4
             if n < NU:
                 x_alloc(n)
             if n in (0, 1):
-                loads_turn(n + 2)
-            if 1 <= n <= NU:
-                interleave(n - 1, 0)
+                loads_turn(n + 2, 0)
+                loads_turn(n + 2, 1)
             for x in range(4):
                 if n < NU:
                     x_scalar(n, x)
-                    x_vector(n, x)
-                if n in (6, 10, 14):
-                    o_exit((n - 6) // 4, x)
+                    if n < NU - 1:
+                        x_vector(n, x)
+                step = 4 * n + x
+                if step >= E_STEP and (step - E_STEP) % 16 < 4 and step - E_STEP < 48:
+                    o_exit((step - E_STEP) // 16, (step - E_STEP) % 16)
                 if n in (0, 1) and x in (1, 2):
-                    loads_exit(n + 2, x - 1, on_scalar=True)
-                if n in (0, 1) and x == 2:
-                    loads_quant(n + 2)
+                    loads_exit(n + 2, x - 1, on_scalar=(n == 0))
                 if n + 1 < NU:
                     s_pass(n + 1, x)
-                if 0 <= n - 2:
-                    o_pass(n - 2, x)
-                if x == 1 and 1 <= n <= NU:
-                    interleave(n - 1, 1)
+                behind = step - O_DELAY
+                if 0 <= behind < 4 * (NU - 1):
+                    o_pass(behind // 4, behind % 4)
+                    if behind // 4 >= WIDE and behind % 4 == 3:
+                        o_exit_narrow(behind // 4)
+            if 1 <= n <= NU and is_diag(n - 1):
+                add_windows(n - 1)
             if n < 12:
                 jb = BLOCK_ORDER[k + 1]
-                if n % 4 == 0:
+                if n == 0:
+                    lag_interleave(jb, 0)
+                    lag_interleave(jb, 1)
+                elif n == 1:
+                    lag_quant(jb)
+                elif n % 4 == 0:
                     lag_alloc(jb)
                     for t in range(4):
-                        lag_widen(jb, t, on_scalar=False)
+                        lag_widen(jb, t, False)
                 elif n % 4 == 1:
                     lag_interleave(jb, 0)
                     lag_interleave(jb, 1)
-                elif n % 4 == 2:
-                    lag_quant(jb, 0)
-                    lag_quant(jb, 1)
-            if 1 <= n <= NU:
-                quant(n - 1, 0)
-                quant(n - 1, 1)
-            if n - 2 >= WIDE:
-                o_exit_narrow(n - 2)
+                elif n % 4 == 2 and n > 2:
+                    lag_quant(jb)
+            if n in (0, 1):
+                loads_quant(n + 2)
+            if 1 <= n < NU - 1:
+                interleave(n - 1)
+            if 2 <= n < NU - 1:
+                quant(n - 2)
+            if n == NU - 1:
+                quant(n - 2)
+                interleave(n - 1)
+                x_vector(n, 1)
+                quant(n - 1)
+            if n == NU:
+                interleave(n - 1, (0, 2))
+                quant(n - 1, 0, 256)
+                interleave(n - 1, (3,))
+                quant(n - 1, 256, 512)
+        finish(NU - 1)

@@ -18,6 +18,19 @@ M, K, R = 2048, 512, 512
 FLOPS = 2 * M * K * M + 2 * R * M * M
 
 P = 128
+PE_LAG = ()
+HALF_UNITS = ()
+DIRECT = {12: (1,), 13: (1,), 14: (1,), 15: (1,)}
+LAG_AT = (((0, 1), (0, 3)), ((0, 3), (1, 1)), ((0, 3), (1, 1)))
+V_OTHER, V_INT, V_Q = 1, 1, 3
+T3_AT = (1, 2)
+T3S = False
+PE_HEAD = False
+ND = 4
+LAG0 = ((3, 4), (0, 1), (1, 2), (2, 3))
+WS0, WS = 0, (0, 1)
+O_D = (14, 14, 14, 10)
+V_SWITCH = 14
 BLOCK_ORDER = (3, 0, 1, 2)
 PITCH = 544
 
@@ -34,18 +47,19 @@ def tile_spike_covariance_readout_s13_kernel(
 
         lagsc = keep.tile([P, 4], F32, name="lagsc")
         nc.scalar.dma_start(out=lagsc[:], in_=lag_scale.rearrange("(p t) o -> p (t o)", t=4))
-        gain_b = keep.tile([P, 4, 4], BF16, name="gain_b")
-        nc.scalar.dma_start(out=gain_b[:], in_=gain.rearrange("(g p t) -> p g t", p=P, t=4))
-        priv_b = keep.tile([P, 4, 4], BF16, name="priv_b")
-        nc.scalar.dma_start(out=priv_b[:], in_=private.rearrange("(g p t) -> p g t", p=P, t=4))
+        gp_rows = keep.tile([P, 512], BF16, name="gp_rows")
+        nc.vector.memset(gp_rows[:].bitcast(I32), 0)
+        nc.scalar.dma_start(out=gp_rows[0:4, :], in_=gain.rearrange("(g x) -> g x", g=4))
+        nc.scalar.dma_start(out=gp_rows[4:8, :], in_=private.rearrange("(g x) -> g x", g=4))
 
         lag_view = lag_bytes.rearrange("(p t) j -> p t j", t=4)
         lag_raw = {}
         raw = {}
 
-        def load_lag(jb):
+        def load_lag(jb, parts=((0, 4),)):
             lraw = work.tile([P, 4, 512], U8, name="lraw", bufs=4, align_bytes=64)
-            nc.sync.dma_start(out=lraw[:], in_=lag_view[:, :, 512 * jb : 512 * jb + 512])
+            for a, b in parts:
+                nc.sync.dma_start(out=lraw[:, a:b, :], in_=lag_view[:, a:b, 512 * jb : 512 * jb + 512])
             lag_raw[jb] = lraw
 
         def load_loads(g, parts):
@@ -56,7 +70,7 @@ def tile_spike_covariance_readout_s13_kernel(
                 nc.sync.dma_start(out=rows[:, a : a + step, :], in_=src[:, a : a + step, :])
             raw[g] = rows
 
-        load_lag(BLOCK_ORDER[0])
+        load_lag(BLOCK_ORDER[0], LAG0)
         load_loads(0, 2)
         load_loads(1, 1)
         load_lag(BLOCK_ORDER[1])
@@ -83,27 +97,21 @@ def tile_spike_covariance_readout_s13_kernel(
         nc.gpsimd.memset(dmini[:].rearrange("p q c t -> p (q c t)").bitcast(I32), 0)
         ident = keep.tile([P, P], F32, name="ident")
         make_identity(nc, ident[:])
-        gain_f = keep.tile([P, 16], F32, name="gain_f")
-        nc.gpsimd.tensor_copy(out=gain_f[:], in_=gain_b[:].rearrange("p g t -> p (g t)"))
-        priv_f = keep.tile([P, 16], F32, name="priv_f")
-        nc.gpsimd.tensor_copy(out=priv_f[:], in_=priv_b[:].rearrange("p g t -> p (g t)"))
+        ident_b = keep.tile([P, P], BF16, name="ident_b")
+        nc.gpsimd.tensor_copy(out=ident_b[:], in_=ident[:])
+        gp_f = keep.tile([P, 2, 16], F32, name="gp_f")
+        gain_f, priv_f = gp_f[:, 0, :], gp_f[:, 1, :]
         diag = keep.tile([P, 16, P], BF16, name="diag")
-        for jb in BLOCK_ORDER[:3]:
+
+        def build_diag(jb):
             for t in range(4):
-                i = 4 * jb + t
-                nc.gpsimd.tensor_scalar(
-                    out=diag[:, i, :], in0=ident[:], scalar1=priv_f[:, i : i + 1], scalar2=0.0, op0=ALU.mult, op1=ALU.add
+                if jb != BLOCK_ORDER[3]:
+                    dst, src = diag[:, 4 * jb + t, :], ident[:]
+                else:
+                    dst, src = dmini[:, :, 32 * t : 32 * t + 32, t], ident[:].rearrange("p (q m) -> p q m", q=4)
+                nc.vector.tensor_scalar(
+                    out=dst, in0=src, scalar1=priv_f[:, 4 * jb + t : 4 * jb + t + 1], scalar2=None, op0=ALU.mult
                 )
-        for t in range(4):
-            i = 4 * BLOCK_ORDER[3] + t
-            nc.gpsimd.tensor_scalar(
-                out=dmini[:, :, 32 * t : 32 * t + 32, t],
-                in0=ident[:].rearrange("p (q m) -> p q m", q=4),
-                scalar1=priv_f[:, i : i + 1],
-                scalar2=0.0,
-                op0=ALU.mult,
-                op1=ALU.add,
-            )
 
         lag_planes, lag_grp, lag_codes, lag_sc = {}, {}, {}, {}
         ld_grp, ld_codes, ld_sc = {}, {}, {}
@@ -127,6 +135,26 @@ def tile_spike_covariance_readout_s13_kernel(
             src = lag_planes[jb][:, :, 256 * h : 256 * h + 256].rearrange("p t (q m s) -> p q m t s", q=2, s=4)
             dst = lag_grp[jb][:, 256 * h : 256 * h + 256, :].rearrange("p (q s m) t -> p q m t s", q=2, s=4)
             nc.vector.tensor_copy(out=dst, in_=src)
+
+        lag_banks = {}
+
+        def lag_turn(jb, h):
+            s_bank = psum.tile([P, 1024], BF16, name="s_bank")
+            lag_banks[jb, h] = s_bank
+            for i in range(2):
+                q = 2 * h + i
+                nc.tensor.matmul(
+                    out=s_bank[:, 512 * i : 512 * i + 512],
+                    lhsT=ident_b[:],
+                    rhs=lag_planes[jb][:, :, 128 * q : 128 * q + 128].rearrange("p t (m s) -> p s m t", s=4),
+                    start=True,
+                    stop=True,
+                )
+
+        def lag_exit(jb, h):
+            nc.scalar.copy(
+                out=lag_grp[jb][:, 256 * h : 256 * h + 256, :].rearrange("p c t -> p (c t)"), in_=lag_banks[jb, h][:]
+            )
 
         def lag_quant(jb):
             nc.vector.quantize_mx(
@@ -177,8 +205,8 @@ def tile_spike_covariance_readout_s13_kernel(
         banks, planes, grouped, codes, scales, wins = {}, {}, {}, {}, {}, {}
         o_banks = {}
 
-        def direct(g):
-            return g == 1
+        def direct(n, g):
+            return g in DIRECT.get(n, ())
 
         def is_diag(n):
             return n < WIDE and units[n][0] == units[n][1]
@@ -187,7 +215,22 @@ def tile_spike_covariance_readout_s13_kernel(
             jb, y = units[n]
             s_bank = psum.tile([P, 512], F32, name="s_bank")
             banks[n, x] = s_bank
-            if n < WIDE:
+            if n in HALF_UNITS:
+                if x % 2 == 0:
+                    ts, c0, w = (x, x + 1), 0, 256
+                else:
+                    ts, c0, w = (0, 1, 2, 3), 256 + 64 * (x - 1), 128
+                for i, t in enumerate(ts):
+                    nc.tensor.matmul_mx(
+                        out=s_bank[:, w * i : w * i + w],
+                        lhsT=ld_codes[y][:, 128 * t : 128 * t + 128].bitcast(FP8X4),
+                        lhsT_scale=ld_sc[y][:, 128 * t : 128 * t + 128],
+                        rhs=lag_codes[jb][:, c0 : c0 + w].bitcast(FP8X4),
+                        rhs_scale=lag_sc[jb][:, c0 : c0 + w],
+                        start=True,
+                        stop=True,
+                    )
+            elif n < WIDE:
                 nc.tensor.matmul_mx(
                     out=s_bank[:],
                     lhsT=ld_codes[y][:, 128 * x : 128 * x + 128].bitcast(FP8X4),
@@ -225,6 +268,12 @@ def tile_spike_covariance_readout_s13_kernel(
         def x_scalar(n, x):
             jb, y = units[n]
             bank = banks[n, x]
+            if n in HALF_UNITS:
+                if x % 2 == 0:
+                    for i in range(2):
+                        t = x + i
+                        exit_scaled(planes[n][:, 512 * t : 512 * t + 256], bank[:, 256 * i : 256 * i + 256], y, t)
+                return
             if n < WIDE:
                 g, t = y, x
                 dst = planes[n][:, 512 * t : 512 * t + 512]
@@ -241,7 +290,7 @@ def tile_spike_covariance_readout_s13_kernel(
                         exit_scaled(d4[:, :, hi:128], b4[:, :, hi:128], g, t)
             else:
                 g = x
-                if direct(g):
+                if direct(n, g):
                     return
                 for t in range(4):
                     c = slice(128 * t, 128 * t + 128)
@@ -249,12 +298,16 @@ def tile_spike_covariance_readout_s13_kernel(
                     exit_scaled(dst, bank[:, c], g, t)
 
         def x_vector(n, x):
-            if n < WIDE or not direct(x):
+            if n in HALF_UNITS and x % 2 == 1:
+                g, a = units[n][1], 1024 + 256 * (x - 1)
+            elif n >= WIDE and direct(n, x):
+                g, a = x, 512 * x
+            else:
                 return
             nc.vector.tensor_tensor(
-                out=grouped[n][:, 512 * x : 512 * x + 512].rearrange("p (c t) -> p c t", t=4),
+                out=grouped[n][:, a : a + 512].rearrange("p (c t) -> p c t", t=4),
                 in0=banks[n, x][:].rearrange("p (t c) -> p c t", t=4),
-                in1=gain_f[:, 4 * x : 4 * x + 4].unsqueeze(1).to_broadcast([P, 128, 4]),
+                in1=gain_f[:, 4 * g : 4 * g + 4].unsqueeze(1).to_broadcast([P, 128, 4]),
                 op=ALU.mult,
             )
 
@@ -271,14 +324,17 @@ def tile_spike_covariance_readout_s13_kernel(
 
         def interleave(n, gs=(0, 1, 2, 3)):
             if n < WIDE:
+                w = 256 if n in HALF_UNITS else 512
                 nc.vector.tensor_copy(
-                    out=grouped[n][:].rearrange("p (c i t) -> p c t i", i=4, t=4),
-                    in_=planes[n][:, 0:2048].rearrange("p (t c i) -> p c t i", t=4, i=4),
+                    out=grouped[n][:, 0 : 4 * w].rearrange("p (c i t) -> p c t i", i=4, t=4),
+                    in_=planes[n][:, 0:2048].rearrange("p (t c) -> p t c", t=4)[:, :, 0:w].rearrange(
+                        "p t (c i) -> p c t i", i=4
+                    ),
                 )
                 return
             jb, q = units[n]
             for g in gs:
-                if direct(g):
+                if direct(n, g):
                     continue
                 dst = grouped[n][:, 512 * g : 512 * g + 512]
                 if g == jb:
@@ -390,83 +446,145 @@ def tile_spike_covariance_readout_s13_kernel(
         lag_widen(jb0, 3, True)
         for t in range(3):
             lag_widen(jb0, t, False)
-        loads_turn(0, 0)
-        loads_exit(0, 0)
-        loads_turn(0, 1)
-        loads_exit(0, 1)
-        lag_interleave(jb0, 0)
-        lag_interleave(jb0, 1)
+        if PE_HEAD:
+            loads_turn(0, 0)
+            lag_turn(jb0, 0)
+            loads_exit(0, 0)
+            lag_exit(jb0, 0)
+            loads_turn(0, 1)
+            lag_turn(jb0, 1)
+            lag_exit(jb0, 1)
+            loads_exit(0, 1)
+        else:
+            loads_turn(0, 0)
+            loads_exit(0, 0)
+            loads_turn(0, 1)
+            loads_exit(0, 1)
+            lag_interleave(jb0, 0)
+            lag_interleave(jb0, 1)
         loads_quant(0, 0, 256)
         lag_quant(jb0)
         loads_quant(0, 256, 512)
         for h in range(2):
             loads_turn(1, h)
             loads_exit(1, h)
+        o_bank = psum.tile([P, 1024], BF16, name="o_bank")
+        for t in range(4):
+            nc.tensor.transpose(o_bank[:, 128 * t : 128 * t + 128], gp_rows[:, t:512:4], ident_b[:])
+        nc.scalar.copy(
+            out=gp_f[:].rearrange("p a (g t) -> p a g t", t=4),
+            in_=o_bank[:, 0:512].rearrange("p (t r) -> p t r", t=4)[:, :, 0:8].rearrange("p t (a g) -> p a g t", a=2),
+        )
         lag_alloc(BLOCK_ORDER[1])
         for t in range(4):
-            lag_widen(BLOCK_ORDER[1], t, False)
+            lag_widen(BLOCK_ORDER[1], t, t < WS0)
         loads_quant(1)
-        for x in range(4):
-            s_pass(0, x)
 
-        O_DELAY = 14
-        E_STEP = 16 + O_DELAY
-        for n in range(NU + 3):
-            k = n // 4
-            if n < NU:
-                x_alloc(n)
-            if n in (0, 1):
-                loads_turn(n + 2, 0)
-                loads_turn(n + 2, 1)
+        jobs = []
+        for n in range(NU):
             for x in range(4):
-                if n < NU:
-                    x_scalar(n, x)
-                    if n < NU - 1:
-                        x_vector(n, x)
-                step = 4 * n + x
-                if step >= E_STEP and (step - E_STEP) % 16 < 4 and step - E_STEP < 48:
-                    o_exit((step - E_STEP) // 16, (step - E_STEP) % 16)
-                if n in (0, 1) and x in (1, 2):
-                    loads_exit(n + 2, x - 1, on_scalar=(n == 0))
-                if n + 1 < NU:
-                    s_pass(n + 1, x)
-                behind = step - O_DELAY
-                if 0 <= behind < 4 * (NU - 1):
-                    o_pass(behind // 4, behind % 4)
-                    if behind // 4 >= WIDE and behind % 4 == 3:
-                        o_exit_narrow(behind // 4)
-            if 1 <= n <= NU and is_diag(n - 1):
+                jobs.append(("unit", n, x))
+                k = n // 4
+                if n < 12 and k in PE_LAG and (n % 4, x) in LAG_AT[k]:
+                    jobs.append(("lag", k, LAG_AT[k].index((n % 4, x))))
+
+        def fill(job):
+            kind, a, b = job
+            if kind == "lag":
+                lag_turn(BLOCK_ORDER[a + 1], b)
+            else:
+                s_pass(a, b)
+
+        def vector_work(n, x):
+            k = n // 4
+            if n == 0:
+                if x == 1:
+                    lag_interleave(BLOCK_ORDER[1], 0)
+                    lag_interleave(BLOCK_ORDER[1], 1)
+                    for jb in BLOCK_ORDER[:ND]:
+                        build_diag(jb)
+                if x == 2:
+                    loads_quant(2)
+                if x == 3:
+                    if not T3S:
+                        loads_exit(3, 0, on_scalar=False)
+                        loads_exit(3, 1, on_scalar=False)
+                    lag_quant(BLOCK_ORDER[1])
+                    if not T3S:
+                        loads_quant(3)
+                return
+            if T3S and n == 1 and x == 1:
+                loads_quant(3)
+            if x == 0 and is_diag(n - 1):
                 add_windows(n - 1)
-            if n < 12:
-                jb = BLOCK_ORDER[k + 1]
-                if n == 0:
-                    lag_interleave(jb, 0)
-                    lag_interleave(jb, 1)
-                elif n == 1:
-                    lag_quant(jb)
-                elif n % 4 == 0:
+            if x == V_OTHER:
+                if n in (2, 4, 5) and {2: 1, 4: 2, 5: 3}[n] >= ND:
+                    build_diag(BLOCK_ORDER[{2: 1, 4: 2, 5: 3}[n]])
+                if n in (3, 7):
+                    jb = BLOCK_ORDER[k + 2]
                     lag_alloc(jb)
                     for t in range(4):
-                        lag_widen(jb, t, False)
-                elif n % 4 == 1:
-                    lag_interleave(jb, 0)
-                    lag_interleave(jb, 1)
-                elif n % 4 == 2 and n > 2:
-                    lag_quant(jb)
-            if n in (0, 1):
-                loads_quant(n + 2)
-            if 1 <= n < NU - 1:
+                        lag_widen(jb, t, t < WS[k])
+                if n in (5, 9) and k not in PE_LAG:
+                    lag_interleave(BLOCK_ORDER[k + 1], 0)
+                    lag_interleave(BLOCK_ORDER[k + 1], 1)
+                if n in (6, 10):
+                    lag_quant(BLOCK_ORDER[k + 1])
+            if x == V_INT:
                 interleave(n - 1)
-            if 2 <= n < NU - 1:
-                quant(n - 2)
-            if n == NU - 1:
-                quant(n - 2)
-                interleave(n - 1)
-                x_vector(n, 1)
-                quant(n - 1)
-            if n == NU:
-                interleave(n - 1, (0, 2))
-                quant(n - 1, 0, 256)
-                interleave(n - 1, (3,))
-                quant(n - 1, 256, 512)
+            if x == V_Q:
+                if n < V_SWITCH and n >= 2:
+                    quant(n - 2)
+                if n == V_SWITCH:
+                    quant(n - 2)
+                if n >= V_SWITCH:
+                    quant(n - 1)
+
+        o_done = [0]
+
+        def out_passes(step, most):
+            for i in range(most):
+                o = o_done[0]
+                if o >= 4 * (NU - 1) or o + O_D[o // 16] > step:
+                    return
+                if o % 16 < 4 and o >= 16:
+                    o_exit(o // 16 - 1, o % 16)
+                o_pass(o // 4, o % 4)
+                if o // 4 >= WIDE and o % 4 == 3:
+                    o_exit_narrow(o // 4)
+                o_done[0] = o + 1
+
+        for job in jobs[:4]:
+            fill(job)
+        loads_turn(2, 0)
+        loads_turn(2, 1)
+        step = 0
+        for j, (kind, n, x) in enumerate(jobs):
+            if kind == "lag":
+                lag_exit(BLOCK_ORDER[n + 1], x)
+                if j + 4 < len(jobs):
+                    fill(jobs[j + 4])
+                continue
+            if x == 0:
+                x_alloc(n)
+            x_scalar(n, x)
+            x_vector(n, x)
+            if n == 0 and x in (1, 2):
+                loads_exit(2, x - 1)
+            if T3S and step in (3, 5):
+                loads_exit(3, (step - 3) // 2)
+            if j + 4 < len(jobs):
+                fill(jobs[j + 4])
+            if n == 0 and x in T3_AT:
+                loads_turn(3, T3_AT.index(x))
+            vector_work(n, x)
+            out_passes(step, 2)
+            step += 1
+        if V_SWITCH > NU - 1:
+            quant(NU - 2)
+        interleave(NU - 1, (0, 1, 2))
+        quant(NU - 1, 0, 256)
+        interleave(NU - 1, (3,))
+        quant(NU - 1, 256, 512)
+        out_passes(1000, 1000)
         finish(NU - 1)

from contextlib import ExitStack

import concourse.mybir as mybir
from concourse.masks import make_identity

F32 = mybir.dt.float32
BF16 = mybir.dt.bfloat16
U32 = mybir.dt.uint32
I32 = mybir.dt.int32
U8 = mybir.dt.uint8
FP8 = mybir.dt.float8_e4m3fn
FP8X4 = mybir.dt.float8_e4m3fn_x4
FP4X4 = mybir.dt.float4_e2m1fn_x4
ALU = mybir.AluOpType
ACT = mybir.ActivationFunctionType

M, K, R = 2048, 512, 512
FLOPS = 2 * M * K * M + 2 * R * M * M

P = 128
PE_LAG = ()
HALF_UNITS = ()
DIRECT = {12: (1,), 13: (1,), 14: (1,), 15: (1,)}
LAG_AT = (((0, 1), (0, 3)), ((0, 3), (1, 1)), ((0, 3), (1, 1)))
V_OTHER, V_INT, V_Q = 1, 1, 3
T3_AT = (1, 2)
T3S = False
PE_HEAD = False
ND = 4
LAG0 = ((3, 4), (0, 1), (1, 2), (2, 3))
WS0, WS = 0, (0, 1)
O_D = (14, 14, 14, 10)
V_SWITCH = 14
BLOCK_ORDER = (3, 0, 1, 2)
PITCH = 544


def tile_spike_covariance_readout_s13_kernel(
    tc, loads, lag_bytes, lag_scale, gain, private, w_words, w_scales, out
):
    nc = tc.nc
    with ExitStack() as ctx:
        keep = ctx.enter_context(tc.tile_pool(name="keep", bufs=1))
        work = ctx.enter_context(tc.tile_pool(name="work", bufs=3))
        psum = ctx.enter_context(tc.psum_pool(name="psum", bufs=4))
        ctx.enter_context(tc.manual_schedule())

        lagsc = keep.tile([P, 4], F32, name="lagsc")
        nc.scalar.dma_start(out=lagsc[:], in_=lag_scale.rearrange("(p t) o -> p (t o)", t=4))
        gp_rows = keep.tile([P, 512], BF16, name="gp_rows")
        nc.vector.memset(gp_rows[:].bitcast(I32), 0)
        nc.scalar.dma_start(out=gp_rows[0:4, :], in_=gain.rearrange("(g x) -> g x", g=4))
        nc.scalar.dma_start(out=gp_rows[4:8, :], in_=private.rearrange("(g x) -> g x", g=4))

        lag_view = lag_bytes.rearrange("(p t) j -> p t j", t=4)
        lag_raw = {}
        raw = {}

        def load_lag(jb, parts=((0, 4),)):
            lraw = work.tile([P, 4, 512], U8, name="lraw", bufs=4, align_bytes=64)
            for a, b in parts:
                nc.sync.dma_start(out=lraw[:, a:b, :], in_=lag_view[:, a:b, 512 * jb : 512 * jb + 512])
            lag_raw[jb] = lraw

        def load_loads(g, parts):
            rows = work.tile([P, 4, 512], BF16, name="rows", bufs=4, align_bytes=64)
            src = loads[512 * g : 512 * g + 512, :].rearrange("(m t) k -> m t k", t=4)
            step = 4 // parts
            for a in range(0, 4, step):
                nc.sync.dma_start(out=rows[:, a : a + step, :], in_=src[:, a : a + step, :])
            raw[g] = rows

        load_lag(BLOCK_ORDER[0], LAG0)
        load_loads(0, 2)
        load_loads(1, 1)
        load_lag(BLOCK_ORDER[1])
        load_loads(2, 1)
        load_loads(3, 1)
        w_sb = keep.tile([P, 4, 1024], U8, name="w_sb", align_bytes=64)
        nc.sync.dma_start(out=w_sb[:], in_=w_words.rearrange("g p n -> p g n"))
        ws_sb = keep.tile([P, 4, 512], U8, name="ws_sb", align_bytes=64)
        nc.vector.memset(ws_sb[:].rearrange("p g n -> p (g n)").bitcast(I32), 0)
        ws_view = w_scales.bitcast(I32).rearrange("g q n -> q g n")
        for quad in range(4):
            nc.sync.dma_start(
                out=ws_sb[32 * quad : 32 * quad + 4, :, :].bitcast(I32),
                in_=ws_view[4 * quad : 4 * quad + 4, :, :],
            )
        load_lag(BLOCK_ORDER[2])
        load_lag(BLOCK_ORDER[3])

        warm = keep.tile([P, 1], F32, name="warm")
        nc.gpsimd.memset(warm[:], 0.0)
        warm2 = keep.tile([P, 1], F32, name="warm2")
        nc.scalar.activation(out=warm2[:], in_=warm[:], func=ACT.Copy, scale=1.0)
        dmini = keep.tile([P, 4, 128, 4], BF16, name="dmini")
        nc.gpsimd.memset(dmini[:].rearrange("p q c t -> p (q c t)").bitcast(I32), 0)
        ident = keep.tile([P, P], F32, name="ident")
        make_identity(nc, ident[:])
        ident_b = keep.tile([P, P], BF16, name="ident_b")
        nc.gpsimd.tensor_copy(out=ident_b[:], in_=ident[:])
        gp_f = keep.tile([P, 2, 16], F32, name="gp_f")
        gain_f, priv_f = gp_f[:, 0, :], gp_f[:, 1, :]
        diag = keep.tile([P, 16, P], BF16, name="diag")

        def build_diag(jb):
            for t in range(4):
                if jb != BLOCK_ORDER[3]:
                    dst, src = diag[:, 4 * jb + t, :], ident[:]
                else:
                    dst, src = dmini[:, :, 32 * t : 32 * t + 32, t], ident[:].rearrange("p (q m) -> p q m", q=4)
                nc.vector.tensor_scalar(
                    out=dst, in0=src, scalar1=priv_f[:, 4 * jb + t : 4 * jb + t + 1], scalar2=None, op0=ALU.mult
                )

        lag_planes, lag_grp, lag_codes, lag_sc = {}, {}, {}, {}
        ld_grp, ld_codes, ld_sc = {}, {}, {}

        def lag_alloc(jb):
            lpl = work.tile([P, 4, 512], BF16, name="lpl", bufs=2, align_bytes=64)
            lgr = work.tile([P, 512, 4], BF16, name="lgr", bufs=2, align_bytes=64)
            lco = work.tile([P, 512], U32, name="lco", bufs=2, align_bytes=64)
            lsc = work.tile([P, 512], U8, name="lsc", bufs=2, align_bytes=64)
            lag_planes[jb], lag_grp[jb], lag_codes[jb], lag_sc[jb] = lpl, lgr, lco, lsc

        def lag_widen(jb, t, on_scalar):
            src = lag_raw[jb][:, t, :].bitcast(FP8)
            dst = lag_planes[jb][:, t, :]
            if on_scalar:
                nc.scalar.activation(out=dst, in_=src, func=ACT.Copy, scale=lagsc[:, t : t + 1])
            else:
                nc.vector.tensor_scalar(out=dst, in0=src, scalar1=lagsc[:, t : t + 1], scalar2=None, op0=ALU.mult)

        def lag_interleave(jb, h):
            src = lag_planes[jb][:, :, 256 * h : 256 * h + 256].rearrange("p t (q m s) -> p q m t s", q=2, s=4)
            dst = lag_grp[jb][:, 256 * h : 256 * h + 256, :].rearrange("p (q s m) t -> p q m t s", q=2, s=4)
            nc.vector.tensor_copy(out=dst, in_=src)

        lag_banks = {}

        def lag_turn(jb, h):
            s_bank = psum.tile([P, 1024], BF16, name="s_bank")
            lag_banks[jb, h] = s_bank
            for i in range(2):
                q = 2 * h + i
                nc.tensor.matmul(
                    out=s_bank[:, 512 * i : 512 * i + 512],
                    lhsT=ident_b[:],
                    rhs=lag_planes[jb][:, :, 128 * q : 128 * q + 128].rearrange("p t (m s) -> p s m t", s=4),
                    start=True,
                    stop=True,
                )

        def lag_exit(jb, h):
            nc.scalar.copy(
                out=lag_grp[jb][:, 256 * h : 256 * h + 256, :].rearrange("p c t -> p (c t)"), in_=lag_banks[jb, h][:]
            )

        def lag_quant(jb):
            nc.vector.quantize_mx(
                out=lag_codes[jb][:].bitcast(FP8X4),
                scales=lag_sc[jb][:],
                in_=lag_grp[jb][:].rearrange("p c t -> p (c t)"),
            )

        turned = {}

        def loads_turn(g, h):
            if h == 0:
                lg = work.tile([P, 512, 4], BF16, name="lg", bufs=2, align_bytes=64)
                lc = work.tile([P, 512], U32, name="lc", bufs=4, align_bytes=64)
                ls = work.tile([P, 512], U8, name="ls", bufs=4, align_bytes=64)
                ld_grp[g], ld_codes[g], ld_sc[g] = lg, lc, ls
            o_bank = psum.tile([P, 512], F32, name="o_bank")
            view = o_bank[:].rearrange("p (t u m) -> p t u m", t=2, u=2)
            for tt in range(2):
                words = raw[g][:, 2 * h + tt, :].bitcast(F32)
                for u in range(2):
                    nc.tensor.transpose(view[:, tt, u, :], words[:, u:256:2], ident[:])
            turned[g, h] = o_bank

        def loads_exit(g, h, on_scalar=True):
            src = turned[g, h][:].rearrange("p (t u m) -> p t m u", t=2, u=2)
            dst = (
                ld_grp[g][:, 256 * h : 256 * h + 256, :]
                .rearrange("p c t -> p (c t)")
                .bitcast(F32)
                .rearrange("p (t m u) -> p t m u", t=2, u=2)
            )
            if on_scalar:
                nc.scalar.copy(out=dst, in_=src)
            else:
                nc.vector.tensor_copy(out=dst, in_=src)

        def loads_quant(g, lo=0, hi=512):
            nc.vector.quantize_mx(
                out=ld_codes[g][:, lo:hi].bitcast(FP8X4),
                scales=ld_sc[g][:, lo:hi],
                in_=ld_grp[g][:, lo:hi, :].rearrange("p c t -> p (c t)"),
            )

        units = [(jb, g) for jb in BLOCK_ORDER[:3] for g in range(4)] + [(BLOCK_ORDER[3], q) for q in range(4)]
        NU = len(units)
        WIDE = 12
        banks, planes, grouped, codes, scales, wins = {}, {}, {}, {}, {}, {}
        o_banks = {}

        def direct(n, g):
            return g in DIRECT.get(n, ())

        def is_diag(n):
            return n < WIDE and units[n][0] == units[n][1]

        def s_pass(n, x):
            jb, y = units[n]
            s_bank = psum.tile([P, 512], F32, name="s_bank")
            banks[n, x] = s_bank
            if n in HALF_UNITS:
                if x % 2 == 0:
                    ts, c0, w = (x, x + 1), 0, 256
                else:
                    ts, c0, w = (0, 1, 2, 3), 256 + 64 * (x - 1), 128
                for i, t in enumerate(ts):
                    nc.tensor.matmul_mx(
                        out=s_bank[:, w * i : w * i + w],
                        lhsT=ld_codes[y][:, 128 * t : 128 * t + 128].bitcast(FP8X4),
                        lhsT_scale=ld_sc[y][:, 128 * t : 128 * t + 128],
                        rhs=lag_codes[jb][:, c0 : c0 + w].bitcast(FP8X4),
                        rhs_scale=lag_sc[jb][:, c0 : c0 + w],
                        start=True,
                        stop=True,
                    )
            elif n < WIDE:
                nc.tensor.matmul_mx(
                    out=s_bank[:],
                    lhsT=ld_codes[y][:, 128 * x : 128 * x + 128].bitcast(FP8X4),
                    lhsT_scale=ld_sc[y][:, 128 * x : 128 * x + 128],
                    rhs=lag_codes[jb][:].bitcast(FP8X4),
                    rhs_scale=lag_sc[jb][:],
                    start=True,
                    stop=True,
                )
            else:
                for t in range(4):
                    nc.tensor.matmul_mx(
                        out=s_bank[:, 128 * t : 128 * t + 128],
                        lhsT=ld_codes[x][:, 128 * t : 128 * t + 128].bitcast(FP8X4),
                        lhsT_scale=ld_sc[x][:, 128 * t : 128 * t + 128],
                        rhs=lag_codes[jb][:, 128 * y : 128 * y + 128].bitcast(FP8X4),
                        rhs_scale=lag_sc[jb][:, 128 * y : 128 * y + 128],
                        start=True,
                        stop=True,
                    )

        def x_alloc(n):
            pl = work.tile([P, 4 * PITCH], BF16, name="pl", bufs=4, align_bytes=64)
            gr = work.tile([P, 2048], BF16, name="gr", bufs=4, align_bytes=64)
            co = work.tile([P, 512], U32, name="co", bufs=4, align_bytes=64)
            sc = work.tile([P, 512], U8, name="sc", bufs=4, align_bytes=64)
            planes[n], grouped[n], codes[n], scales[n] = pl, gr, co, sc
            if is_diag(n) or n >= WIDE:
                win = work.tile([P, 4, 128], F32, name="win", bufs=2)
                wins[n] = win

        def exit_scaled(dst, src, g, t):
            nc.scalar.activation(out=dst, in_=src, func=ACT.Copy, scale=gain_f[:, 4 * g + t : 4 * g + t + 1])

        def x_scalar(n, x):
            jb, y = units[n]
            bank = banks[n, x]
            if n in HALF_UNITS:
                if x % 2 == 0:
                    for i in range(2):
                        t = x + i
                        exit_scaled(planes[n][:, 512 * t : 512 * t + 256], bank[:, 256 * i : 256 * i + 256], y, t)
                return
            if n < WIDE:
                g, t = y, x
                dst = planes[n][:, 512 * t : 512 * t + 512]
                if g != jb:
                    exit_scaled(dst, bank[:], g, t)
                else:
                    b4 = bank[:].rearrange("p (q c) -> p q c", q=4)
                    d4 = dst.rearrange("p (q c) -> p q c", q=4)
                    lo, hi = 32 * t, 32 * t + 32
                    exit_scaled(wins[n][:, t, :].rearrange("p (q c) -> p q c", q=4), b4[:, :, lo:hi], g, t)
                    if t > 0:
                        exit_scaled(d4[:, :, 0:lo], b4[:, :, 0:lo], g, t)
                    if t < 3:
                        exit_scaled(d4[:, :, hi:128], b4[:, :, hi:128], g, t)
            else:
                g = x
                if direct(n, g):
                    return
                for t in range(4):
                    c = slice(128 * t, 128 * t + 128)
                    dst = wins[n][:, t, :] if g == jb else planes[n][:, 512 * g + 128 * t : 512 * g + 128 * t + 128]
                    exit_scaled(dst, bank[:, c], g, t)

        def x_vector(n, x):
            if n in HALF_UNITS and x % 2 == 1:
                g, a = units[n][1], 1024 + 256 * (x - 1)
            elif n >= WIDE and direct(n, x):
                g, a = x, 512 * x
            else:
                return
            nc.vector.tensor_tensor(
                out=grouped[n][:, a : a + 512].rearrange("p (c t) -> p c t", t=4),
                in0=banks[n, x][:].rearrange("p (t c) -> p c t", t=4),
                in1=gain_f[:, 4 * g : 4 * g + 4].unsqueeze(1).to_broadcast([P, 128, 4]),
                op=ALU.mult,
            )

        def add_windows(n):
            g = units[n][1]
            nc.vector.tensor_tensor(
                out=planes[n][:].rearrange("p (t c) -> p t c", t=4)[:, :, 0:512].rearrange("p t (q c) -> p t q c", q=4)[
                    :, :, :, 0:32
                ],
                in0=wins[n][:].rearrange("p t (q c) -> p t q c", q=4),
                in1=diag[:, 4 * g : 4 * g + 4, :].rearrange("p t (q c) -> p t q c", q=4),
                op=ALU.add,
            )

        def interleave(n, gs=(0, 1, 2, 3)):
            if n < WIDE:
                w = 256 if n in HALF_UNITS else 512
                nc.vector.tensor_copy(
                    out=grouped[n][:, 0 : 4 * w].rearrange("p (c i t) -> p c t i", i=4, t=4),
                    in_=planes[n][:, 0:2048].rearrange("p (t c) -> p t c", t=4)[:, :, 0:w].rearrange(
                        "p t (c i) -> p c t i", i=4
                    ),
                )
                return
            jb, q = units[n]
            for g in gs:
                if direct(n, g):
                    continue
                dst = grouped[n][:, 512 * g : 512 * g + 512]
                if g == jb:
                    nc.vector.tensor_tensor(
                        out=dst.rearrange("p (c t) -> p c t", t=4),
                        in0=wins[n][:].rearrange("p t c -> p c t"),
                        in1=dmini[:, q, :, :],
                        op=ALU.add,
                    )
                else:
                    nc.vector.tensor_copy(
                        out=dst.rearrange("p (c i t) -> p c t i", i=4, t=4),
                        in_=planes[n][:, 512 * g : 512 * g + 512].rearrange("p (t c i) -> p c t i", t=4, i=4),
                    )

        def quant(n, lo=0, hi=512):
            nc.vector.quantize_mx(
                out=codes[n][:, lo:hi].bitcast(FP8X4), scales=scales[n][:, lo:hi], in_=grouped[n][:, 4 * lo : 4 * hi]
            )

        def w_op(g, r):
            return w_sb[:, g, 256 * r : 256 * r + 256].bitcast(FP4X4), ws_sb[:, g, 128 * r : 128 * r + 128]

        def o_pass(n, r):
            jb, y = units[n]
            if n < WIDE:
                if y == 0:
                    o_bank = psum.tile([P, 512], F32, name="o_bank")
                    o_banks[n // 4, r] = o_bank
                wc, ws = w_op(y, r)
                nc.tensor.matmul_mx(
                    out=o_banks[n // 4, r][:],
                    lhsT=wc,
                    lhsT_scale=ws,
                    rhs=codes[n][:].bitcast(FP8X4),
                    rhs_scale=scales[n][:],
                    start=(y == 0),
                    stop=(y == 3),
                )
            else:
                if r == 0:
                    o_bank = psum.tile([P, 512], F32, name="o_bank")
                    o_banks[n, 0] = o_bank
                for g in range(4):
                    wc, ws = w_op(g, r)
                    nc.tensor.matmul_mx(
                        out=o_banks[n, 0][:, 128 * r : 128 * r + 128],
                        lhsT=wc,
                        lhsT_scale=ws,
                        rhs=codes[n][:, 128 * g : 128 * g + 128].bitcast(FP8X4),
                        rhs_scale=scales[n][:, 128 * g : 128 * g + 128],
                        start=(g == 0),
                        stop=(g == 3),
                    )

        def o_exit(k, r):
            jb = BLOCK_ORDER[k]
            ot = work.tile([P, 512], F32, name="ot", bufs=8)
            nc.scalar.copy(
                out=ot[:].rearrange("p (q m s) -> p q m s", q=4, s=4),
                in_=o_banks[k, r][:].rearrange("p (q s m) -> p q m s", q=4, s=4),
            )
            nc.sync.dma_start(out=out[128 * r : 128 * r + 128, 512 * jb : 512 * jb + 512], in_=ot[:])

        def o_exit_narrow(n):
            jb, q = units[n]
            j0 = 512 * jb + 128 * q
            ot = work.tile([P, 512], F32, name="ot", bufs=8)
            dst = ot[:].rearrange("p (r m s) -> p r m s", r=4, s=4)
            src = o_banks[n, 0][:].rearrange("p (r s m) -> p r m s", r=4, s=4)
            hbm = out[:, j0 : j0 + 128].rearrange("(r p) j -> p r j", p=P)
            o3 = ot[:].rearrange("p (r j) -> p r j", r=4)
            nc.scalar.copy(out=dst, in_=src)
            nc.sync.dma_start(out=hbm, in_=o3)

        def finish(n):
            jb, q = units[n]
            j0 = 512 * jb + 128 * q
            accs = []
            for r in range(4):
                s_bank = psum.tile([P, 512], F32, name="s_bank")
                accs.append(s_bank)
            for g in range(4):
                for r in range(4):
                    wc, ws = w_op(g, r)
                    nc.tensor.matmul_mx(
                        out=accs[r][:, 0:128],
                        lhsT=wc,
                        lhsT_scale=ws,
                        rhs=codes[n][:, 128 * g : 128 * g + 128].bitcast(FP8X4),
                        rhs_scale=scales[n][:, 128 * g : 128 * g + 128],
                        start=(g == 0),
                        stop=(g == 3),
                    )
            ot = work.tile([P, 512], F32, name="ot", bufs=8)
            o3 = ot[:].rearrange("p (r j) -> p r j", r=4)
            hbm = out[:, j0 : j0 + 128].rearrange("(r p) j -> p r j", p=P)
            for r in range(4):
                dst = o3[:, r, :].rearrange("p (m s) -> p m s", s=4)
                src = accs[r][:, 0:128].rearrange("p (s m) -> p m s", s=4)
                if r % 2 == 0:
                    nc.scalar.copy(out=dst, in_=src)
                else:
                    nc.vector.tensor_copy(out=dst, in_=src)
                    nc.sync.dma_start(out=hbm[:, r - 1 : r + 1], in_=o3[:, r - 1 : r + 1])

        jb0 = BLOCK_ORDER[0]
        lag_alloc(jb0)
        lag_widen(jb0, 3, True)
        for t in range(3):
            lag_widen(jb0, t, False)
        if PE_HEAD:
            loads_turn(0, 0)
            lag_turn(jb0, 0)
            loads_exit(0, 0)
            lag_exit(jb0, 0)
            loads_turn(0, 1)
            lag_turn(jb0, 1)
            lag_exit(jb0, 1)
            loads_exit(0, 1)
        else:
            loads_turn(0, 0)
            loads_exit(0, 0)
            loads_turn(0, 1)
            loads_exit(0, 1)
            lag_interleave(jb0, 0)
            lag_interleave(jb0, 1)
        loads_quant(0, 0, 256)
        lag_quant(jb0)
        loads_quant(0, 256, 512)
        for h in range(2):
            loads_turn(1, h)
            loads_exit(1, h)
        o_bank = psum.tile([P, 1024], BF16, name="o_bank")
        for t in range(4):
            nc.tensor.transpose(o_bank[:, 128 * t : 128 * t + 128], gp_rows[:, t:512:4], ident_b[:])
        nc.scalar.copy(
            out=gp_f[:].rearrange("p a (g t) -> p a g t", t=4),
            in_=o_bank[:, 0:512].rearrange("p (t r) -> p t r", t=4)[:, :, 0:8].rearrange("p t (a g) -> p a g t", a=2),
        )
        lag_alloc(BLOCK_ORDER[1])
        for t in range(4):
            lag_widen(BLOCK_ORDER[1], t, t < WS0)
        loads_quant(1)

        jobs = []
        for n in range(NU):
            for x in range(4):
                jobs.append(("unit", n, x))
                k = n // 4
                if n < 12 and k in PE_LAG and (n % 4, x) in LAG_AT[k]:
                    jobs.append(("lag", k, LAG_AT[k].index((n % 4, x))))

        def fill(job):
            kind, a, b = job
            if kind == "lag":
                lag_turn(BLOCK_ORDER[a + 1], b)
            else:
                s_pass(a, b)

        def vector_work(n, x):
            k = n // 4
            if n == 0:
                if x == 1:
                    lag_interleave(BLOCK_ORDER[1], 0)
                    lag_interleave(BLOCK_ORDER[1], 1)
                    for jb in BLOCK_ORDER[:ND]:
                        build_diag(jb)
                if x == 2:
                    loads_quant(2)
                if x == 3:
                    if not T3S:
                        loads_exit(3, 0, on_scalar=False)
                        loads_exit(3, 1, on_scalar=False)
                    lag_quant(BLOCK_ORDER[1])
                    if not T3S:
                        loads_quant(3)
                return
            if T3S and n == 1 and x == 1:
                loads_quant(3)
            if x == 0 and is_diag(n - 1):
                add_windows(n - 1)
            if x == V_OTHER:
                if n in (2, 4, 5) and {2: 1, 4: 2, 5: 3}[n] >= ND:
                    build_diag(BLOCK_ORDER[{2: 1, 4: 2, 5: 3}[n]])
                if n in (3, 7):
                    jb = BLOCK_ORDER[k + 2]
                    lag_alloc(jb)
                    for t in range(4):
                        lag_widen(jb, t, t < WS[k])
                if n in (5, 9) and k not in PE_LAG:
                    lag_interleave(BLOCK_ORDER[k + 1], 0)
                    lag_interleave(BLOCK_ORDER[k + 1], 1)
                if n in (6, 10):
                    lag_quant(BLOCK_ORDER[k + 1])
            if x == V_INT:
                interleave(n - 1)
            if x == V_Q:
                if n < V_SWITCH and n >= 2:
                    quant(n - 2)
                if n == V_SWITCH:
                    quant(n - 2)
                if n >= V_SWITCH:
                    quant(n - 1)

        o_done = [0]

        def out_passes(step, most):
            for i in range(most):
                o = o_done[0]
                if o >= 4 * (NU - 1) or o + O_D[o // 16] > step:
                    return
                if o % 16 < 4 and o >= 16:
                    o_exit(o // 16 - 1, o % 16)
                o_pass(o // 4, o % 4)
                if o // 4 >= WIDE and o % 4 == 3:
                    o_exit_narrow(o // 4)
                o_done[0] = o + 1

        for job in jobs[:4]:
            fill(job)
        loads_turn(2, 0)
        loads_turn(2, 1)
        step = 0
        for j, (kind, n, x) in enumerate(jobs):
            if kind == "lag":
                lag_exit(BLOCK_ORDER[n + 1], x)
                if j + 4 < len(jobs):
                    fill(jobs[j + 4])
                continue
            if x == 0:
                x_alloc(n)
            x_scalar(n, x)
            x_vector(n, x)
            if n == 0 and x in (1, 2):
                loads_exit(2, x - 1)
            if T3S and step in (3, 5):
                loads_exit(3, (step - 3) // 2)
            if j + 4 < len(jobs):
                fill(jobs[j + 4])
            if n == 0 and x in T3_AT:
                loads_turn(3, T3_AT.index(x))
            vector_work(n, x)
            out_passes(step, 2)
            step += 1
        if V_SWITCH > NU - 1:
            quant(NU - 2)
        interleave(NU - 1, (0, 1, 2))
        quant(NU - 1, 0, 256)
        interleave(NU - 1, (3,))
        quant(NU - 1, 256, 512)
        out_passes(1000, 1000)
        finish(NU - 1)
